import numpy as np
import ml_dtypes


def mxq(x, axis, fmt="e4m3"):
    dtype, down = {"e4m3": (ml_dtypes.float8_e4m3fn, 7), "e5m2": (ml_dtypes.float8_e5m2, 14)}[fmt]
    v = np.moveaxis(np.asarray(x, np.float32).astype(ml_dtypes.bfloat16).astype(np.float64), axis, -1)
    blocks = v.reshape(v.shape[:-1] + (-1, 32))
    amax = np.abs(blocks).max(-1, keepdims=True)
    byte = np.maximum(np.where(amax > 0, np.frexp(amax)[1] - 1 + 127, 0) - down, 1)
    scale = np.exp2(byte - 127.0)
    codes = (blocks / scale).astype(np.float32).astype(dtype).astype(np.float64)
    return np.moveaxis((codes * scale).reshape(v.shape), -1, axis)


WIDE = False


def mx_kscale(k):
    if not WIDE:
        return np.ones(k)
    levels = np.array([10, -10, 5, -5, 0])
    if k % 512:
        return np.exp2(np.random.permutation(np.resize(levels, k // 32))).repeat(32)
    a = np.empty((k // 512, 16))
    for p in range(k // 512):
        a[p, :8] = np.random.permutation(np.resize(levels, 8))
        for g in range(8):
            far = levels[np.abs(levels - a[p, g]) >= 10]
            a[p, g + 8] = far[np.random.randint(len(far))]
    return np.exp2(a.ravel()).repeat(32)


def f64(x):
    return np.asarray(x).astype(np.float64)


def striped(idx):
    return np.tile(idx.reshape(-1, 16).T, (8, 1)).astype(np.uint16)


def unstriped(offs):
    return offs[:16].T.reshape(-1).astype(np.int64)


def striped8(idx):
    return np.concatenate([x.reshape(-1, 16).T for x in idx]).astype(np.uint16)


def runs(offs, k):
    lists = np.stack([offs[16 * r : 16 * r + 16].T.reshape(-1) for r in range(8)]).astype(np.int64)
    return lists[np.arange(k) % 512 // 64]


def pack_weight(w):
    k, n = w.shape
    w = f64(np.asarray(w, np.float32).astype(ml_dtypes.bfloat16)).reshape(k // 32, 32, n)
    amax = np.abs(w).max(1)
    byte = np.clip(np.where(amax > 0, np.frexp(amax)[1] - 1 + 127 - 7, 1), 1, 254)
    scaled = (w * np.exp2(127.0 - byte)[:, None, :]).reshape(k, n).astype(np.float32)
    words = np.ascontiguousarray(scaled.reshape(k // 512, 128, 4, n).transpose(0, 1, 3, 2)).astype(ml_dtypes.float8_e4m3fn).view(np.uint8)
    return words, np.ascontiguousarray(byte.astype(np.uint8).reshape(k // 512, 16, n))


def unpack_weight(words, scales):
    g, p, n, _ = words.shape
    vals = np.ascontiguousarray(words).view(ml_dtypes.float8_e4m3fn).astype(np.float64) * np.repeat(np.exp2(scales.astype(np.float64) - 127.0), 8, axis=1)[..., None]
    return vals.transpose(0, 1, 3, 2).reshape(g * 512, n)


def relu(v):
    return np.maximum(v, 0.0)


K, T, S, N, H = 512, 2048, 512, 512, 512


def setup_inputs():
    n = np.random.standard_normal
    s = mx_kscale(K)[:, None]
    u = mx_kscale(H)
    packed_xT = pack_weight(n((K, T)) * s)
    return {
        "x_words": packed_xT[0],
        "x_scales": packed_xT[1],
        "w1": (n((K, H)) / np.sqrt(K) / s).astype(np.float32),
        "w2": (n((K, H)) / np.sqrt(K) / s).astype(np.float32),
        "gn": (np.random.uniform(0.5, 1.5, (H, 1)) * u[:, None]).astype(np.float32),
        "w3": (n((H, N)) / np.sqrt(H) / u[:, None]).astype(np.float32),
        "offs": striped(np.random.permutation(T)[:S]),
        "two": striped(np.random.permutation(T)[:S]),
        "n1": striped8(np.stack([np.random.permutation(S) for _ in range(8)])),
        "n2": striped8(np.stack([np.random.permutation(S) for _ in range(8)])),
        "n3": striped8(np.stack([np.random.permutation(S) for _ in range(8)])),
        "n4": striped8(np.stack([np.random.permutation(S) for _ in range(8)])),
    }


def reference(x_words, x_scales, w1, w2, gn, w3, offs, two, n1, n2, n3, n4):
    xq = unpack_weight(x_words, x_scales)[:, unstriped(offs)]
    y = mxq(f64(w1), 0, "e4m3").T @ xq
    x_two = unpack_weight(x_words, x_scales)[:, unstriped(two)]
    d = mxq(f64(w2), 0, "e4m3").T @ x_two
    z = f64(gn) * (y[np.arange(H)[:, None], runs(n1, H)] - (np.tanh(d) * (d[np.arange(H)[:, None], runs(n2, H)])))
    h = mxq(f64(w3), 0, "e4m3").T @ mxq(z, 0, "e4m3")
    return relu(h - (h[np.arange(N)[:, None], runs(n3, N)])) + 0.5 * (relu(h[np.arange(N)[:, None], runs(n4, N)] - h))

@@ -1,0 +1,158 @@
+from contextlib import ExitStack
+
+import concourse.mybir as mybir
+
+K, T, S, N, H = 512, 2048, 512, 512, 512
+FLOPS = 3 * 2 * 512 * 512 * 512
+
+F32 = mybir.dt.float32
+BF16 = mybir.dt.bfloat16
+U32 = mybir.dt.uint32
+I32 = mybir.dt.int32
+U16 = mybir.dt.uint16
+U8 = mybir.dt.uint8
+FP8X4 = mybir.dt.float8_e4m3fn_x4
+ACT = mybir.ActivationFunctionType
+ALU = mybir.AluOpType
+
+P = 128
+PACK = 4
+RUN = 8
+BLOCKS = 16
+WINDOW = 2 * S
+CHUNKS = (256, 256)
+
+
+def tile_picked_twlsoftbhinge_none_p_kernel(
+    tc, x_words, x_scales, w1, w2, gn, w3, offs, two, n1, n2, n3, n4, out
+):
+    nc = tc.nc
+    with ExitStack() as ctx:
+        keep = ctx.enter_context(tc.tile_pool(name="keep", bufs=1))
+        psum = ctx.enter_context(tc.psum_pool(name="psum", bufs=1))
+
+        def sb(shape, dtype, name):
+            return keep.tile(shape, dtype, name=name, align_bytes=64)
+
+        lists = {name: sb([P, S // 16], U16, "list_" + name) for name in ("offs", "two", "n1", "n2", "n3", "n4")}
+        word_table = sb([P, T], U32, "word_table")
+        byte_table = sb([P, T], U8, "byte_table")
+        gain = [sb([P, 1], F32, "gain%d" % t) for t in range(PACK)]
+        raw = {name: sb([P, PACK, H], F32, "raw_" + name) for name in ("w1", "w2")}
+        raw3 = sb([P, PACK, N], F32, "raw_w3")
+
+        nc.vector.memset(byte_table[:].bitcast(I32), 0)
+        nc.sync.dma_start(out=lists["two"][:], in_=two)
+        nc.sync.dma_start(out=word_table[:].bitcast(I32), in_=x_words[0].rearrange("p n t -> p (n t)").bitcast(I32))
+        for q in range(4):
+            nc.scalar.dma_start(
+                out=byte_table[32 * q : 32 * q + 4, :].bitcast(I32), in_=x_scales[0, 4 * q : 4 * q + 4, :].bitcast(I32)
+            )
+        nc.sync.dma_start(out=lists["offs"][:], in_=offs)
+        nc.sync.dma_start(out=raw["w2"][:], in_=w2.rearrange("(p j) c -> p j c", j=PACK))
+        with nc.allow_non_contiguous_dma(reason="one gain a feature"):
+            for t in range(PACK):
+                nc.gpsimd.dma_start(out=gain[t][:], in_=gn.rearrange("(b t q) o -> t b q o", t=PACK, q=RUN)[t])
+        nc.sync.dma_start(out=raw["w1"][:], in_=w1.rearrange("(p j) c -> p j c", j=PACK))
+        nc.sync.dma_start(out=lists["n2"][:], in_=n2)
+        nc.sync.dma_start(out=lists["n1"][:], in_=n1)
+        w3_rows = w3.rearrange("(b t q) c -> t b q c", t=PACK, q=RUN)
+        for t in range(PACK):
+            nc.sync.dma_start(out=raw3[:, t, :], in_=w3_rows[t])
+        nc.sync.dma_start(out=lists["n3"][:], in_=n3)
+        nc.sync.dma_start(out=lists["n4"][:], in_=n4)
+
+        d_window = [sb([P, WINDOW], F32, "d_window%d" % t) for t in range(PACK)]
+        y_window = [sb([P, WINDOW], F32, "y_window%d" % t) for t in range(PACK)]
+        h_window = [sb([P, WINDOW], F32, "h_window%d" % t) for t in range(PACK)]
+        for window in d_window + h_window:
+            nc.vector.memset(window[:, S:], 0.0)
+
+        picked = {}
+        for name in ("two", "offs"):
+            words = sb([P, S], U32, "words_" + name)
+            scales = sb([P, S], U8, "scales_" + name)
+            nc.vector.tensor_copy(words[:], word_table[:].indirect(lists[name][:]))
+            nc.vector.tensor_copy(scales[:], byte_table[:].indirect(lists[name][:]))
+            picked[name] = (words, scales)
+
+        def deal(source, t, name):
+            grouped = sb([P, P * PACK], BF16, "grouped_%s%d" % (name, t))
+            nc.scalar.copy(
+                out=grouped[:].rearrange("p (b q j) -> p b q j", q=RUN, j=PACK),
+                in_=source[:].rearrange("p j (b t q) -> p t b q j", t=PACK, q=RUN)[:, t],
+            )
+            return grouped
+
+        def quantise(grouped, width, name):
+            words = sb([P, width], U32, "qwords_" + name)
+            scales = sb([P, width], U8, "qscales_" + name)
+            nc.vector.quantize_mx(out=words[:].bitcast(FP8X4), scales=scales[:], in_=grouped[:])
+            return words, scales
+
+        def product(bank, weights, moving):
+            nc.tensor.matmul_mx(
+                out=bank,
+                lhsT=weights[0][:].bitcast(FP8X4),
+                lhsT_scale=weights[1][:],
+                rhs=moving[0][:].bitcast(FP8X4),
+                rhs_scale=moving[1][:],
+                start=True,
+                stop=True,
+            )
+
+        banks = [psum.tile([P, S], F32, name="bank%d" % b) for b in range(8)]
+
+        damped = []
+        for t in range(PACK):
+            product(banks[t][:], quantise(deal(raw["w2"], t, "w2"), P, "w2_%d" % t), picked["two"])
+            nc.scalar.activation(d_window[t][:, :S], banks[t][:], ACT.Copy, scale=gain[t][:])
+            nc.scalar.activation(y_window[t][:, S:], banks[t][:], ACT.Tanh)
+            term = sb([P, S], F32, "damped%d" % t)
+            nc.vector.tensor_tensor(term[:], d_window[t][:].indirect(lists["n2"][:]), y_window[t][:, S:], ALU.mult)
+            damped.append(term)
+        for t in range(PACK):
+            product(banks[4 + t][:], quantise(deal(raw["w1"], t, "w1"), P, "w1_%d" % t), picked["offs"])
+            nc.scalar.activation(y_window[t][:, :S], banks[4 + t][:], ACT.Copy, scale=gain[t][:])
+        w3_tiles = [quantise(deal(raw3, t, "w3"), P, "w3_%d" % t) for t in range(PACK)]
+
+        h_plain = sb([P, PACK, S], F32, "h_plain")
+        first = 0
+        bank_at = 0
+        for c, width in enumerate(CHUNKS):
+            cols = slice(first, first + width)
+            z = sb([P, PACK, width], F32, "z%d" % c)
+            for t in range(PACK):
+                nc.vector.tensor_tensor(
+                    z[:, t, :],
+                    y_window[t][:].indirect(lists["n1"][:, first // 16 : (first + width) // 16]),
+                    damped[t][:, cols],
+                    ALU.subtract,
+                )
+            grouped = sb([P, width * PACK], BF16, "grouped_z%d" % c)
+            nc.scalar.copy(out=grouped[:].rearrange("p (n j) -> p n j", j=PACK), in_=z[:].rearrange("p j n -> p n j"))
+            z_tile = quantise(grouped, width, "z%d" % c)
+            per_bank = S // width
+            for t0 in range(0, PACK, per_bank):
+                bank = banks[bank_at]
+                bank_at = bank_at + 1
+                for t in range(t0, t0 + per_bank):
+                    product(bank[:, (t - t0) * width : (t - t0 + 1) * width], w3_tiles[t], z_tile)
+                for t in range(t0, t0 + per_bank):
+                    nc.scalar.activation(h_window[t][:, cols], bank[:, (t - t0) * width : (t - t0 + 1) * width], ACT.Copy, scale=0.5)
+                nc.scalar.activation(
+                    h_plain[:, t0 : t0 + per_bank, cols], bank[:].rearrange("p (t n) -> p t n", n=width), ACT.Copy, scale=0.5
+                )
+            first = first + width
+
+        out_rows = out.rearrange("(b t q) c -> t b q c", t=PACK, q=RUN)
+        for t in range(PACK):
+            below = sb([P, S], F32, "below%d" % t)
+            above = sb([P, S], F32, "above%d" % t)
+            hinge = sb([P, S], F32, "hinge%d" % t)
+            result = sb([P, S], F32, "result%d" % t)
+            nc.vector.tensor_tensor(below[:], h_window[t][:].indirect(lists["n3"][:]), h_plain[:, t, :], ALU.subtract)
+            nc.vector.tensor_tensor(above[:], h_window[t][:].indirect(lists["n4"][:]), h_plain[:, t, :], ALU.subtract)
+            nc.scalar.activation(hinge[:], below[:], ACT.Relu, scale=-2.0)
+            nc.vector.scalar_tensor_tensor(result[:], above[:], 0.0, hinge[:], ALU.max, ALU.add)
+            nc.sync.dma_start(out=out_rows[t], in_=result[:])

@@ -20,7 +20,8 @@ PACK = 4
 RUN = 8
 BLOCKS = 16
 WINDOW = 2 * S
-CHUNKS = (256, 256)
+CHUNKS = (256, 128, 128)
+LINE = 4
 
 
 def tile_picked_twlsoftbhinge_none_p_kernel(
@@ -31,30 +32,32 @@ def tile_picked_twlsoftbhinge_none_p_kernel(
         keep = ctx.enter_context(tc.tile_pool(name="keep", bufs=1))
         psum = ctx.enter_context(tc.psum_pool(name="psum", bufs=1))
 
-        def sb(shape, dtype, name):
-            return keep.tile(shape, dtype, name=name, align_bytes=64)
+        def sb(shape, dtype, name, tag=None):
+            return keep.tile(shape, dtype, name=name, tag=tag or name, align_bytes=64)
 
         lists = {name: sb([P, S // 16], U16, "list_" + name) for name in ("offs", "two", "n1", "n2", "n3", "n4")}
         word_table = sb([P, T], U32, "word_table")
         byte_table = sb([P, T], U8, "byte_table")
         gain = [sb([P, 1], F32, "gain%d" % t) for t in range(PACK)]
-        raw = {name: sb([P, PACK, H], F32, "raw_" + name) for name in ("w1", "w2")}
+        raw1 = sb([P, PACK, H], F32, "raw_w1")
+        raw2 = sb([P, PACK, H], F32, "raw_w2")
         raw3 = sb([P, PACK, N], F32, "raw_w3")
 
         nc.vector.memset(byte_table[:].bitcast(I32), 0)
         nc.sync.dma_start(out=lists["two"][:], in_=two)
-        nc.sync.dma_start(out=word_table[:].bitcast(I32), in_=x_words[0].rearrange("p n t -> p (n t)").bitcast(I32))
+        nc.sync.dma_start(out=lists["offs"][:], in_=offs)
+        nc.sync.dma_start(out=lists["n2"][:], in_=n2)
         for q in range(4):
-            nc.scalar.dma_start(
+            queue = nc.sync if q < 2 else nc.scalar
+            queue.dma_start(
                 out=byte_table[32 * q : 32 * q + 4, :].bitcast(I32), in_=x_scales[0, 4 * q : 4 * q + 4, :].bitcast(I32)
             )
-        nc.sync.dma_start(out=lists["offs"][:], in_=offs)
-        nc.sync.dma_start(out=raw["w2"][:], in_=w2.rearrange("(p j) c -> p j c", j=PACK))
-        with nc.allow_non_contiguous_dma(reason="one gain a feature"):
+        nc.sync.dma_start(out=raw2[:], in_=w2.rearrange("(p j) c -> p j c", j=PACK))
+        nc.sync.dma_start(out=word_table[:].bitcast(I32), in_=x_words[0].rearrange("p n t -> p (n t)").bitcast(I32))
+        with nc.allow_non_contiguous_dma(reason="one gain a partition"):
             for t in range(PACK):
-                nc.gpsimd.dma_start(out=gain[t][:], in_=gn.rearrange("(b t q) o -> t b q o", t=PACK, q=RUN)[t])
-        nc.sync.dma_start(out=raw["w1"][:], in_=w1.rearrange("(p j) c -> p j c", j=PACK))
-        nc.sync.dma_start(out=lists["n2"][:], in_=n2)
+                nc.sync.dma_start(out=gain[t][:], in_=gn.rearrange("(b t q) o -> t b q o", t=PACK, q=RUN)[t])
+        nc.sync.dma_start(out=raw1[:], in_=w1.rearrange("(p j) c -> p j c", j=PACK))
         nc.sync.dma_start(out=lists["n1"][:], in_=n1)
         w3_rows = w3.rearrange("(b t q) c -> t b q c", t=PACK, q=RUN)
         for t in range(PACK):
@@ -63,65 +66,83 @@ def tile_picked_twlsoftbhinge_none_p_kernel(
         nc.sync.dma_start(out=lists["n4"][:], in_=n4)
 
         d_window = [sb([P, WINDOW], F32, "d_window%d" % t) for t in range(PACK)]
-        y_window = [sb([P, WINDOW], F32, "y_window%d" % t) for t in range(PACK)]
+        y_window = [sb([P, S], F32, "y_window%d" % t) for t in range(PACK)]
         h_window = [sb([P, WINDOW], F32, "h_window%d" % t) for t in range(PACK)]
-        for window in d_window + h_window:
+        for window in d_window + h_window[1:]:
             nc.vector.memset(window[:, S:], 0.0)
+        nc.scalar.activation(h_window[0][:, S:], d_window[0][:, S:], ACT.Tanh)
 
-        picked = {}
-        for name in ("two", "offs"):
-            words = sb([P, S], U32, "words_" + name)
-            scales = sb([P, S], U8, "scales_" + name)
-            nc.vector.tensor_copy(words[:], word_table[:].indirect(lists[name][:]))
-            nc.vector.tensor_copy(scales[:], byte_table[:].indirect(lists[name][:]))
-            picked[name] = (words, scales)
-
-        def deal(source, t, name):
-            grouped = sb([P, P * PACK], BF16, "grouped_%s%d" % (name, t))
-            nc.scalar.copy(
-                out=grouped[:].rearrange("p (b q j) -> p b q j", q=RUN, j=PACK),
-                in_=source[:].rearrange("p j (b t q) -> p t b q j", t=PACK, q=RUN)[:, t],
+        def deal(copy, source, t, name, tag=None):
+            grouped = sb([P, P * PACK], BF16, "grouped_%s%d" % (name, t), tag)
+            copy(
+                out=grouped[:].rearrange("p (b c i j) -> p b c j i", c=RUN // LINE, i=LINE, j=PACK),
+                in_=source[:].rearrange("p j (b t c i) -> p t b c j i", t=PACK, c=RUN // LINE, i=LINE)[:, t],
             )
             return grouped
 
-        def quantise(grouped, width, name):
-            words = sb([P, width], U32, "qwords_" + name)
-            scales = sb([P, width], U8, "qscales_" + name)
+        def quantise_weights(grouped, name):
+            words = sb([P, P], U32, "qwords_" + name)
+            scales = sb([P, P], U8, "qscales_" + name)
             nc.vector.quantize_mx(out=words[:].bitcast(FP8X4), scales=scales[:], in_=grouped[:])
             return words, scales
 
-        def product(bank, weights, moving):
+        def product(bank, weights, words, scales):
             nc.tensor.matmul_mx(
                 out=bank,
                 lhsT=weights[0][:].bitcast(FP8X4),
                 lhsT_scale=weights[1][:],
-                rhs=moving[0][:].bitcast(FP8X4),
-                rhs_scale=moving[1][:],
+                rhs=words.bitcast(FP8X4),
+                rhs_scale=scales,
                 start=True,
                 stop=True,
             )
 
+        two_words = sb([P, S], U32, "words_two")
+        two_scales = sb([P, S], U8, "scales_two")
+        offs_words = sb([P, S], U32, "words_offs")
+        offs_scales = sb([P, S], U8, "scales_offs")
+        nc.vector.tensor_copy(two_scales[:], byte_table[:].indirect(lists["two"][:]))
+        nc.vector.tensor_copy(offs_scales[:], byte_table[:].indirect(lists["offs"][:]))
+        w2_tiles = [quantise_weights(deal(nc.scalar.copy, raw2, t, "w2"), "w2_%d" % t) for t in range(PACK)]
+        halves = [slice(0, S // 2), slice(S // 2, S)]
+        for cols in halves:
+            nc.vector.tensor_copy(
+                two_words[:, cols], word_table[:].indirect(lists["two"][:, cols.start // 16 : cols.stop // 16])
+            )
+        nc.vector.tensor_copy(offs_words[:], word_table[:].indirect(lists["offs"][:]))
+
         banks = [psum.tile([P, S], F32, name="bank%d" % b) for b in range(8)]
+        y_banks = [banks[5], banks[6], banks[7], banks[4]]
 
         damped = []
         for t in range(PACK):
-            product(banks[t][:], quantise(deal(raw["w2"], t, "w2"), P, "w2_%d" % t), picked["two"])
-            nc.scalar.activation(d_window[t][:, :S], banks[t][:], ACT.Copy, scale=gain[t][:])
-            nc.scalar.activation(y_window[t][:, S:], banks[t][:], ACT.Tanh)
+            gate = sb([P, S], F32, "gate%d" % t)
+            if t == 0:
+                parts = [(banks[0][:, halves[0]], halves[0]), (banks[4][:, halves[1]], halves[1])]
+            else:
+                parts = [(banks[t][:], slice(0, S))]
+            for bank, cols in parts:
+                product(bank, w2_tiles[t], two_words[:, cols], two_scales[:, cols])
+                nc.scalar.activation(d_window[t][:, cols], bank, ACT.Copy, scale=gain[t][:])
+                nc.scalar.activation(gate[:, cols], bank, ACT.Tanh)
             term = sb([P, S], F32, "damped%d" % t)
-            nc.vector.tensor_tensor(term[:], d_window[t][:].indirect(lists["n2"][:]), y_window[t][:, S:], ALU.mult)
+            nc.vector.tensor_tensor(term[:], d_window[t][:].indirect(lists["n2"][:]), gate[:], ALU.mult)
             damped.append(term)
+            copy = nc.vector.tensor_copy if t == 0 else nc.scalar.copy
+            weights = quantise_weights(deal(copy, raw1, t, "w1"), "w1_%d" % t)
+            product(y_banks[t][:], weights, offs_words[:], offs_scales[:])
         for t in range(PACK):
-            product(banks[4 + t][:], quantise(deal(raw["w1"], t, "w1"), P, "w1_%d" % t), picked["offs"])
-            nc.scalar.activation(y_window[t][:, :S], banks[4 + t][:], ACT.Copy, scale=gain[t][:])
-        w3_tiles = [quantise(deal(raw3, t, "w3"), P, "w3_%d" % t) for t in range(PACK)]
+            nc.scalar.activation(y_window[t][:], y_banks[t][:], ACT.Copy, scale=gain[t][:])
+        w3_first = quantise_weights(deal(nc.scalar.copy, raw3, 0, "w3"), "w3_0")
 
-        h_plain = sb([P, PACK, S], F32, "h_plain")
+        h_plain = [sb([P, S], F32, "h_plain%d" % t) for t in range(PACK)]
+        z_words = sb([P, S], U32, "z_words")
+        z_scales = sb([P, S], U8, "z_scales")
         first = 0
-        bank_at = 0
+        last = len(CHUNKS) - 1
         for c, width in enumerate(CHUNKS):
             cols = slice(first, first + width)
-            z = sb([P, PACK, width], F32, "z%d" % c)
+            z = sb([P, PACK, width], F32, "z%d" % c, "grouped_z0" if c == last else None)
             for t in range(PACK):
                 nc.vector.tensor_tensor(
                     z[:, t, :],
@@ -130,29 +151,49 @@ def tile_picked_twlsoftbhinge_none_p_kernel(
                     ALU.subtract,
                 )
             grouped = sb([P, width * PACK], BF16, "grouped_z%d" % c)
-            nc.scalar.copy(out=grouped[:].rearrange("p (n j) -> p n j", j=PACK), in_=z[:].rearrange("p j n -> p n j"))
-            z_tile = quantise(grouped, width, "z%d" % c)
-            per_bank = S // width
-            for t0 in range(0, PACK, per_bank):
-                bank = banks[bank_at]
-                bank_at = bank_at + 1
-                for t in range(t0, t0 + per_bank):
-                    product(bank[:, (t - t0) * width : (t - t0 + 1) * width], w3_tiles[t], z_tile)
-                for t in range(t0, t0 + per_bank):
-                    nc.scalar.activation(h_window[t][:, cols], bank[:, (t - t0) * width : (t - t0 + 1) * width], ACT.Copy, scale=0.5)
-                nc.scalar.activation(
-                    h_plain[:, t0 : t0 + per_bank, cols], bank[:].rearrange("p (t n) -> p t n", n=width), ACT.Copy, scale=0.5
-                )
+            copy = nc.vector.tensor_copy if c == last else nc.scalar.copy
+            copy(
+                out=grouped[:].rearrange("p (n i j) -> p n j i", i=LINE, j=PACK),
+                in_=z[:].rearrange("p j (n i) -> p n j i", i=LINE),
+            )
+            nc.vector.quantize_mx(out=z_words[:, cols].bitcast(FP8X4), scales=z_scales[:, cols], in_=grouped[:])
+            product(banks[c][:, :width], w3_first, z_words[:, cols], z_scales[:, cols])
+            nc.scalar.activation(h_window[0][:, cols], banks[c][:, :width], ACT.Copy, scale=0.5)
+            nc.scalar.activation(h_plain[0][:, cols], banks[c][:, :width], ACT.Copy, scale=0.5)
             first = first + width
+
+        h_banks = [None, banks[3], banks[5], banks[6]]
+
+        def project(t):
+            weights = quantise_weights(deal(nc.vector.tensor_copy, raw3, t, "w3", "damped%d" % t), "w3_%d" % t)
+            product(h_banks[t][:], weights, z_words[:], z_scales[:])
+
+        def release(t):
+            nc.scalar.activation(h_window[t][:, :S], h_banks[t][:], ACT.Copy, scale=0.5)
+            nc.scalar.activation(h_plain[t][:], h_banks[t][:], ACT.Copy, scale=0.5)
+
+        for t in range(1, PACK):
+            project(t)
 
         out_rows = out.rearrange("(b t q) c -> t b q c", t=PACK, q=RUN)
         for t in range(PACK):
+            if t + 1 < PACK:
+                release(t + 1)
             below = sb([P, S], F32, "below%d" % t)
-            above = sb([P, S], F32, "above%d" % t)
             hinge = sb([P, S], F32, "hinge%d" % t)
-            result = sb([P, S], F32, "result%d" % t)
-            nc.vector.tensor_tensor(below[:], h_window[t][:].indirect(lists["n3"][:]), h_plain[:, t, :], ALU.subtract)
-            nc.vector.tensor_tensor(above[:], h_window[t][:].indirect(lists["n4"][:]), h_plain[:, t, :], ALU.subtract)
+            nc.vector.tensor_tensor(below[:], h_window[t][:].indirect(lists["n3"][:]), h_plain[t][:], ALU.subtract)
             nc.scalar.activation(hinge[:], below[:], ACT.Relu, scale=-2.0)
-            nc.vector.scalar_tensor_tensor(result[:], above[:], 0.0, hinge[:], ALU.max, ALU.add)
-            nc.sync.dma_start(out=out_rows[t], in_=result[:])
+            pieces = 2 if t == PACK - 1 else 1
+            width = S // pieces
+            for piece in range(pieces):
+                cols = slice(piece * width, (piece + 1) * width)
+                above = sb([P, width], F32, "above%d_%d" % (t, piece))
+                result = sb([P, width], F32, "result%d_%d" % (t, piece))
+                nc.vector.tensor_tensor(
+                    above[:],
+                    h_window[t][:].indirect(lists["n4"][:, piece * width // 16 : (piece + 1) * width // 16]),
+                    h_plain[t][:, cols],
+                    ALU.subtract,
+                )
+                nc.vector.scalar_tensor_tensor(result[:], above[:], 0.0, hinge[:, cols], ALU.max, ALU.add)
+                nc.sync.dma_start(out=out_rows[t][:, :, cols], in_=result[:])

@@ -38,12 +38,13 @@ def tile_picked_twlsoftbhinge_none_p_kernel(
         lists = {name: sb([P, S // 16], U16, "list_" + name) for name in ("offs", "two", "n1", "n2", "n3", "n4")}
         word_table = sb([P, T], U32, "word_table")
         byte_table = sb([P, T], U8, "byte_table")
-        gain = [sb([P, 1], F32, "gain%d" % t) for t in range(PACK)]
+        gain_rows = sb([P, P], F32, "gain_rows")
         raw1 = sb([P, PACK, H], F32, "raw_w1")
         raw2 = sb([P, PACK, H], F32, "raw_w2")
         raw3 = sb([P, PACK, N], F32, "raw_w3")
 
         nc.vector.memset(byte_table[:].bitcast(I32), 0)
+        nc.vector.memset(gain_rows[:], 0.0)
         nc.sync.dma_start(out=lists["two"][:], in_=two)
         nc.sync.dma_start(out=lists["offs"][:], in_=offs)
         nc.sync.dma_start(out=lists["n2"][:], in_=n2)
@@ -53,10 +54,8 @@ def tile_picked_twlsoftbhinge_none_p_kernel(
                 out=byte_table[32 * q : 32 * q + 4, :].bitcast(I32), in_=x_scales[0, 4 * q : 4 * q + 4, :].bitcast(I32)
             )
         nc.sync.dma_start(out=raw2[:], in_=w2.rearrange("(p j) c -> p j c", j=PACK))
+        nc.sync.dma_start(out=gain_rows[0:P:32, :], in_=gn.rearrange("(g c) o -> g (c o)", c=P))
         nc.sync.dma_start(out=word_table[:].bitcast(I32), in_=x_words[0].rearrange("p n t -> p (n t)").bitcast(I32))
-        with nc.allow_non_contiguous_dma(reason="one gain a partition"):
-            for t in range(PACK):
-                nc.sync.dma_start(out=gain[t][:], in_=gn.rearrange("(b t q) o -> t b q o", t=PACK, q=RUN)[t])
         nc.sync.dma_start(out=raw1[:], in_=w1.rearrange("(p j) c -> p j c", j=PACK))
         nc.sync.dma_start(out=lists["n1"][:], in_=n1)
         w3_rows = w3.rearrange("(b t q) c -> t b q c", t=PACK, q=RUN)
@@ -68,8 +67,9 @@ def tile_picked_twlsoftbhinge_none_p_kernel(
         d_window = [sb([P, WINDOW], F32, "d_window%d" % t) for t in range(PACK)]
         y_window = [sb([P, S], F32, "y_window%d" % t) for t in range(PACK)]
         h_window = [sb([P, WINDOW], F32, "h_window%d" % t) for t in range(PACK)]
-        for window in d_window + h_window[1:]:
-            nc.vector.memset(window[:, S:], 0.0)
+        gates = [window[:, S:] for window in d_window[1:]] + [sb([P, S], F32, "gate_last")[:]]
+        h_plain = [window[:, S:] for window in h_window[1:]] + [sb([P, S], F32, "h_plain_last")[:]]
+        nc.vector.memset(d_window[0][:, S:], 0.0)
         nc.scalar.activation(h_window[0][:, S:], d_window[0][:, S:], ACT.Tanh)
 
         def deal(copy, source, t, name, tag=None):
@@ -97,13 +97,25 @@ def tile_picked_twlsoftbhinge_none_p_kernel(
                 stop=True,
             )
 
+        gain_dealt = sb([P, P], F32, "gain_dealt")
+        gain_turned = sb([P, P], F32, "gain_turned")
+        nc.vector.tensor_copy(
+            out=gain_dealt[:].rearrange("p (t b q) -> p t b q", t=PACK, q=RUN),
+            in_=gain_rows[:].rearrange("p (b t q) -> p t b q", t=PACK, q=RUN),
+        )
+        nc.vector.transpose(gain_turned[:], gain_dealt[:])
+        gain = [gain_turned[:, 32 * t : 32 * t + 1] for t in range(PACK)]
+
         two_words = sb([P, S], U32, "words_two")
         two_scales = sb([P, S], U8, "scales_two")
         offs_words = sb([P, S], U32, "words_offs")
         offs_scales = sb([P, S], U8, "scales_offs")
         nc.vector.tensor_copy(two_scales[:], byte_table[:].indirect(lists["two"][:]))
         nc.vector.tensor_copy(offs_scales[:], byte_table[:].indirect(lists["offs"][:]))
-        w2_tiles = [quantise_weights(deal(nc.scalar.copy, raw2, t, "w2"), "w2_%d" % t) for t in range(PACK)]
+        w2_tiles = [
+            quantise_weights(deal(nc.vector.tensor_copy if t % 2 == 0 else nc.scalar.copy, raw2, t, "w2"), "w2_%d" % t)
+            for t in range(PACK)
+        ]
         halves = [slice(0, S // 2), slice(S // 2, S)]
         for cols in halves:
             nc.vector.tensor_copy(
@@ -114,28 +126,30 @@ def tile_picked_twlsoftbhinge_none_p_kernel(
         banks = [psum.tile([P, S], F32, name="bank%d" % b) for b in range(8)]
         y_banks = [banks[5], banks[6], banks[7], banks[4]]
 
+        staging = ["staging%d" % t for t in range(PACK)]
         damped = []
         for t in range(PACK):
-            gate = sb([P, S], F32, "gate%d" % t)
+            gate = gates[t]
             if t == 0:
                 parts = [(banks[0][:, halves[0]], halves[0]), (banks[4][:, halves[1]], halves[1])]
             else:
                 parts = [(banks[t][:], slice(0, S))]
             for bank, cols in parts:
                 product(bank, w2_tiles[t], two_words[:, cols], two_scales[:, cols])
-                nc.scalar.activation(d_window[t][:, cols], bank, ACT.Copy, scale=gain[t][:])
+                nc.scalar.activation(d_window[t][:, cols], bank, ACT.Copy, scale=gain[t])
                 nc.scalar.activation(gate[:, cols], bank, ACT.Tanh)
-            term = sb([P, S], F32, "damped%d" % t)
-            nc.vector.tensor_tensor(term[:], d_window[t][:].indirect(lists["n2"][:]), gate[:], ALU.mult)
+            term = sb([P, S], F32, "damped%d" % t, staging[t])
+            nc.vector.tensor_tensor(term[:], d_window[t][:].indirect(lists["n2"][:]), gate, ALU.mult)
             damped.append(term)
-            copy = nc.vector.tensor_copy if t == 0 else nc.scalar.copy
-            weights = quantise_weights(deal(copy, raw1, t, "w1"), "w1_%d" % t)
-            product(y_banks[t][:], weights, offs_words[:], offs_scales[:])
+            if t % 2 == 0:
+                copy = nc.vector.tensor_copy if t == 0 else nc.scalar.copy
+                for u in (t, t + 1):
+                    weights = quantise_weights(deal(copy, raw1, u, "w1", staging[u] if u % 2 else None), "w1_%d" % u)
+                    product(y_banks[u][:], weights, offs_words[:], offs_scales[:])
         for t in range(PACK):
-            nc.scalar.activation(y_window[t][:], y_banks[t][:], ACT.Copy, scale=gain[t][:])
+            nc.scalar.activation(y_window[t][:], y_banks[t][:], ACT.Copy, scale=gain[t])
         w3_first = quantise_weights(deal(nc.scalar.copy, raw3, 0, "w3"), "w3_0")
 
-        h_plain = [sb([P, S], F32, "h_plain%d" % t) for t in range(PACK)]
         z_words = sb([P, S], U32, "z_words")
         z_scales = sb([P, S], U8, "z_scales")
         first = 0
@@ -165,15 +179,24 @@ def tile_picked_twlsoftbhinge_none_p_kernel(
         h_banks = [None, banks[3], banks[5], banks[6]]
 
         def project(t):
-            weights = quantise_weights(deal(nc.vector.tensor_copy, raw3, t, "w3", "damped%d" % t), "w3_%d" % t)
+            grouped = deal(nc.vector.tensor_copy, raw3, t, "w3", staging[t])
+            weights = quantise_weights(grouped, "w3_%d" % t)
             product(h_banks[t][:], weights, z_words[:], z_scales[:])
 
         def release(t):
             nc.scalar.activation(h_window[t][:, :S], h_banks[t][:], ACT.Copy, scale=0.5)
-            nc.scalar.activation(h_plain[t][:], h_banks[t][:], ACT.Copy, scale=0.5)
+            nc.scalar.activation(h_plain[t], h_banks[t][:], ACT.Copy, scale=0.5)
 
         for t in range(1, PACK):
             project(t)
+
+        def hinge_gather(target, t, name, cols):
+            nc.vector.tensor_tensor(
+                target[:, cols],
+                h_window[t][:].indirect(lists[name][:, cols.start // 16 : cols.stop // 16]),
+                h_plain[t][:, cols],
+                ALU.subtract,
+            )
 
         out_rows = out.rearrange("(b t q) c -> t b q c", t=PACK, q=RUN)
         for t in range(PACK):
@@ -181,19 +204,14 @@ def tile_picked_twlsoftbhinge_none_p_kernel(
                 release(t + 1)
             below = sb([P, S], F32, "below%d" % t)
             hinge = sb([P, S], F32, "hinge%d" % t)
-            nc.vector.tensor_tensor(below[:], h_window[t][:].indirect(lists["n3"][:]), h_plain[t][:], ALU.subtract)
+            above = sb([P, S], F32, "above%d" % t, "above%d" % min(t, PACK - 2))
+            for cols in halves if t == 0 else [slice(0, S)]:
+                hinge_gather(below, t, "n3", cols)
             nc.scalar.activation(hinge[:], below[:], ACT.Relu, scale=-2.0)
-            pieces = 2 if t == PACK - 1 else 1
-            width = S // pieces
-            for piece in range(pieces):
-                cols = slice(piece * width, (piece + 1) * width)
-                above = sb([P, width], F32, "above%d_%d" % (t, piece))
-                result = sb([P, width], F32, "result%d_%d" % (t, piece))
-                nc.vector.tensor_tensor(
-                    above[:],
-                    h_window[t][:].indirect(lists["n4"][:, piece * width // 16 : (piece + 1) * width // 16]),
-                    h_plain[t][:, cols],
-                    ALU.subtract,
-                )
-                nc.vector.scalar_tensor_tensor(result[:], above[:], 0.0, hinge[:, cols], ALU.max, ALU.add)
+            pieces = halves if t == PACK - 1 else [slice(0, S)]
+            for cols in pieces:
+                hinge_gather(above, t, "n4", cols)
+            for cols in pieces:
+                result = sb([P, cols.stop - cols.start], F32, "result%d_%d" % (t, cols.start))
+                nc.vector.scalar_tensor_tensor(result[:], above[:, cols], 0.0, hinge[:, cols], ALU.max, ALU.add)
                 nc.sync.dma_start(out=out_rows[t][:, :, cols], in_=result[:])

@@ -1,6 +1,7 @@
 from contextlib import ExitStack
 
 import concourse.mybir as mybir
+from concourse.masks import make_identity
 
 K, T, S, N, H = 512, 2048, 512, 512, 512
 FLOPS = 3 * 2 * 512 * 512 * 512
@@ -22,6 +23,7 @@ BLOCKS = 16
 WINDOW = 2 * S
 CHUNKS = (256, 128, 128)
 LINE = 4
+TURNED = 2
 
 
 def tile_picked_twlsoftbhinge_none_p_kernel(
@@ -71,6 +73,9 @@ def tile_picked_twlsoftbhinge_none_p_kernel(
         h_plain = [window[:, S:] for window in h_window[1:]] + [sb([P, S], F32, "h_plain_last")[:]]
         nc.vector.memset(d_window[0][:, S:], 0.0)
         nc.scalar.activation(h_window[0][:, S:], d_window[0][:, S:], ACT.Tanh)
+
+        identity = sb([P, P], F32, "identity")
+        make_identity(nc, identity[:])
 
         def deal(copy, source, t, name, tag=None):
             grouped = sb([P, P * PACK], BF16, "grouped_%s%d" % (name, t), tag)
@@ -198,20 +203,44 @@ def tile_picked_twlsoftbhinge_none_p_kernel(
                 ALU.subtract,
             )
 
+        def turn(bank, terms):
+            for k in range(S // P):
+                block = slice(k * P, (k + 1) * P)
+                for n, term in enumerate(terms):
+                    nc.tensor.matmul(
+                        bank[:, block], term[:, block], identity[:], is_transpose=True, start=n == 0, stop=n == len(terms) - 1
+                    )
+
+        for t in range(1, PACK):
+            release(t)
+
+        below_banks = [banks[0], banks[2]]
+        above_banks = [banks[1], banks[7]]
+        sum_banks = [banks[4], banks[3]]
         out_rows = out.rearrange("(b t q) c -> t b q c", t=PACK, q=RUN)
         for t in range(PACK):
-            if t + 1 < PACK:
-                release(t + 1)
             below = sb([P, S], F32, "below%d" % t)
-            hinge = sb([P, S], F32, "hinge%d" % t)
             above = sb([P, S], F32, "above%d" % t, "above%d" % min(t, PACK - 2))
             for cols in halves if t == 0 else [slice(0, S)]:
                 hinge_gather(below, t, "n3", cols)
-            nc.scalar.activation(hinge[:], below[:], ACT.Relu, scale=-2.0)
             pieces = halves if t == PACK - 1 else [slice(0, S)]
             for cols in pieces:
                 hinge_gather(above, t, "n4", cols)
-            for cols in pieces:
-                result = sb([P, cols.stop - cols.start], F32, "result%d_%d" % (t, cols.start))
-                nc.vector.scalar_tensor_tensor(result[:], above[:, cols], 0.0, hinge[:, cols], ALU.max, ALU.add)
-                nc.sync.dma_start(out=out_rows[t][:, :, cols], in_=result[:])
+            if t < TURNED:
+                low = sb([P, S], F32, "low%d" % t)
+                high = sb([P, S], F32, "high%d" % t)
+                turn(below_banks[t], [below])
+                nc.scalar.activation(low[:], below_banks[t][:], ACT.Relu, scale=-2.0)
+                turn(above_banks[t], [above])
+                nc.scalar.activation(high[:], above_banks[t][:], ACT.Relu)
+                turn(sum_banks[t], [low, high])
+            else:
+                hinge = sb([P, S], F32, "hinge%d" % t)
+                nc.scalar.activation(hinge[:], below[:], ACT.Relu, scale=-2.0)
+                summed = sb([P, S], F32, "summed%d" % (t - TURNED))
+                nc.scalar.copy(summed[:], sum_banks[t - TURNED][:])
+                nc.sync.dma_start(out=out_rows[t - TURNED], in_=summed[:])
+                for cols in pieces:
+                    result = sb([P, cols.stop - cols.start], F32, "result%d_%d" % (t, cols.start))
+                    nc.vector.scalar_tensor_tensor(result[:], above[:, cols], 0.0, hinge[:, cols], ALU.max, ALU.add)
+                    nc.sync.dma_start(out=out_rows[t][:, :, cols], in_=result[:])

from contextlib import ExitStack

import concourse.mybir as mybir
from concourse.masks import make_identity

K, T, S, N, H = 512, 2048, 512, 512, 512
FLOPS = 3 * 2 * 512 * 512 * 512

F32 = mybir.dt.float32
BF16 = mybir.dt.bfloat16
U32 = mybir.dt.uint32
I32 = mybir.dt.int32
U16 = mybir.dt.uint16
U8 = mybir.dt.uint8
FP8X4 = mybir.dt.float8_e4m3fn_x4
ACT = mybir.ActivationFunctionType
ALU = mybir.AluOpType

P = 128
PACK = 4
RUN = 8
BLOCKS = 16
WINDOW = 2 * S
CHUNKS = (256, 128, 128)
LINE = 4
TURNED = 2


def tile_picked_twlsoftbhinge_none_p_kernel(
    tc, x_words, x_scales, w1, w2, gn, w3, offs, two, n1, n2, n3, n4, out
):
    nc = tc.nc
    with ExitStack() as ctx:
        keep = ctx.enter_context(tc.tile_pool(name="keep", bufs=1))
        psum = ctx.enter_context(tc.psum_pool(name="psum", bufs=1))

        def sb(shape, dtype, name, tag=None):
            return keep.tile(shape, dtype, name=name, tag=tag or name, align_bytes=64)

        lists = {name: sb([P, S // 16], U16, "list_" + name) for name in ("offs", "two", "n1", "n2", "n3", "n4")}
        word_table = sb([P, T], U32, "word_table")
        byte_table = sb([P, T], U8, "byte_table")
        gain_rows = sb([P, P], F32, "gain_rows")
        raw1 = sb([P, PACK, H], F32, "raw_w1")
        raw2 = sb([P, PACK, H], F32, "raw_w2")
        raw3 = sb([P, PACK, N], F32, "raw_w3")

        nc.vector.memset(byte_table[:].bitcast(I32), 0)
        nc.vector.memset(gain_rows[:], 0.0)
        nc.sync.dma_start(out=lists["two"][:], in_=two)
        nc.sync.dma_start(out=lists["offs"][:], in_=offs)
        nc.sync.dma_start(out=lists["n2"][:], in_=n2)
        for q in range(4):
            queue = nc.sync if q < 2 else nc.scalar
            queue.dma_start(
                out=byte_table[32 * q : 32 * q + 4, :].bitcast(I32), in_=x_scales[0, 4 * q : 4 * q + 4, :].bitcast(I32)
            )
        nc.sync.dma_start(out=raw2[:], in_=w2.rearrange("(p j) c -> p j c", j=PACK))
        nc.sync.dma_start(out=gain_rows[0:P:32, :], in_=gn.rearrange("(g c) o -> g (c o)", c=P))
        nc.sync.dma_start(out=word_table[:].bitcast(I32), in_=x_words[0].rearrange("p n t -> p (n t)").bitcast(I32))
        nc.sync.dma_start(out=raw1[:], in_=w1.rearrange("(p j) c -> p j c", j=PACK))
        nc.sync.dma_start(out=lists["n1"][:], in_=n1)
        w3_rows = w3.rearrange("(b t q) c -> t b q c", t=PACK, q=RUN)
        for t in range(PACK):
            nc.sync.dma_start(out=raw3[:, t, :], in_=w3_rows[t])
        nc.sync.dma_start(out=lists["n3"][:], in_=n3)
        nc.sync.dma_start(out=lists["n4"][:], in_=n4)

        d_window = [sb([P, WINDOW], F32, "d_window%d" % t) for t in range(PACK)]
        y_window = [sb([P, S], F32, "y_window%d" % t) for t in range(PACK)]
        h_window = [sb([P, WINDOW], F32, "h_window%d" % t) for t in range(PACK)]
        gates = [window[:, S:] for window in d_window[1:]] + [sb([P, S], F32, "gate_last")[:]]
        h_plain = [window[:, S:] for window in h_window[1:]] + [sb([P, S], F32, "h_plain_last")[:]]
        nc.vector.memset(d_window[0][:, S:], 0.0)
        nc.scalar.activation(h_window[0][:, S:], d_window[0][:, S:], ACT.Tanh)

        identity = sb([P, P], F32, "identity")
        make_identity(nc, identity[:])

        def deal(copy, source, t, name, tag=None):
            grouped = sb([P, P * PACK], BF16, "grouped_%s%d" % (name, t), tag)
            copy(
                out=grouped[:].rearrange("p (b c i j) -> p b c j i", c=RUN // LINE, i=LINE, j=PACK),
                in_=source[:].rearrange("p j (b t c i) -> p t b c j i", t=PACK, c=RUN // LINE, i=LINE)[:, t],
            )
            return grouped

        def quantise_weights(grouped, name):
            words = sb([P, P], U32, "qwords_" + name)
            scales = sb([P, P], U8, "qscales_" + name)
            nc.vector.quantize_mx(out=words[:].bitcast(FP8X4), scales=scales[:], in_=grouped[:])
            return words, scales

        def product(bank, weights, words, scales):
            nc.tensor.matmul_mx(
                out=bank,
                lhsT=weights[0][:].bitcast(FP8X4),
                lhsT_scale=weights[1][:],
                rhs=words.bitcast(FP8X4),
                rhs_scale=scales,
                start=True,
                stop=True,
            )

        gain_dealt = sb([P, P], F32, "gain_dealt")
        gain_turned = sb([P, P], F32, "gain_turned")
        nc.vector.tensor_copy(
            out=gain_dealt[:].rearrange("p (t b q) -> p t b q", t=PACK, q=RUN),
            in_=gain_rows[:].rearrange("p (b t q) -> p t b q", t=PACK, q=RUN),
        )
        nc.vector.transpose(gain_turned[:], gain_dealt[:])
        gain = [gain_turned[:, 32 * t : 32 * t + 1] for t in range(PACK)]

        two_words = sb([P, S], U32, "words_two")
        two_scales = sb([P, S], U8, "scales_two")
        offs_words = sb([P, S], U32, "words_offs")
        offs_scales = sb([P, S], U8, "scales_offs")
        nc.vector.tensor_copy(two_scales[:], byte_table[:].indirect(lists["two"][:]))
        nc.vector.tensor_copy(offs_scales[:], byte_table[:].indirect(lists["offs"][:]))
        w2_tiles = [
            quantise_weights(deal(nc.vector.tensor_copy if t % 2 == 0 else nc.scalar.copy, raw2, t, "w2"), "w2_%d" % t)
            for t in range(PACK)
        ]
        halves = [slice(0, S // 2), slice(S // 2, S)]
        for cols in halves:
            nc.vector.tensor_copy(
                two_words[:, cols], word_table[:].indirect(lists["two"][:, cols.start // 16 : cols.stop // 16])
            )
        nc.vector.tensor_copy(offs_words[:], word_table[:].indirect(lists["offs"][:]))

        banks = [psum.tile([P, S], F32, name="bank%d" % b) for b in range(8)]
        y_banks = [banks[5], banks[6], banks[7], banks[4]]

        staging = ["staging%d" % t for t in range(PACK)]
        damped = []
        for t in range(PACK):
            gate = gates[t]
            if t == 0:
                parts = [(banks[0][:, halves[0]], halves[0]), (banks[4][:, halves[1]], halves[1])]
            else:
                parts = [(banks[t][:], slice(0, S))]
            for bank, cols in parts:
                product(bank, w2_tiles[t], two_words[:, cols], two_scales[:, cols])
                nc.scalar.activation(d_window[t][:, cols], bank, ACT.Copy, scale=gain[t])
                nc.scalar.activation(gate[:, cols], bank, ACT.Tanh)
            term = sb([P, S], F32, "damped%d" % t, staging[t])
            nc.vector.tensor_tensor(term[:], d_window[t][:].indirect(lists["n2"][:]), gate, ALU.mult)
            damped.append(term)
            if t % 2 == 0:
                copy = nc.vector.tensor_copy if t == 0 else nc.scalar.copy
                for u in (t, t + 1):
                    weights = quantise_weights(deal(copy, raw1, u, "w1", staging[u] if u % 2 else None), "w1_%d" % u)
                    product(y_banks[u][:], weights, offs_words[:], offs_scales[:])
        for t in range(PACK):
            nc.scalar.activation(y_window[t][:], y_banks[t][:], ACT.Copy, scale=gain[t])
        w3_first = quantise_weights(deal(nc.scalar.copy, raw3, 0, "w3"), "w3_0")

        z_words = sb([P, S], U32, "z_words")
        z_scales = sb([P, S], U8, "z_scales")
        first = 0
        last = len(CHUNKS) - 1
        for c, width in enumerate(CHUNKS):
            cols = slice(first, first + width)
            z = sb([P, PACK, width], F32, "z%d" % c, "grouped_z0" if c == last else None)
            for t in range(PACK):
                nc.vector.tensor_tensor(
                    z[:, t, :],
                    y_window[t][:].indirect(lists["n1"][:, first // 16 : (first + width) // 16]),
                    damped[t][:, cols],
                    ALU.subtract,
                )
            grouped = sb([P, width * PACK], BF16, "grouped_z%d" % c)
            copy = nc.vector.tensor_copy if c == last else nc.scalar.copy
            copy(
                out=grouped[:].rearrange("p (n i j) -> p n j i", i=LINE, j=PACK),
                in_=z[:].rearrange("p j (n i) -> p n j i", i=LINE),
            )
            nc.vector.quantize_mx(out=z_words[:, cols].bitcast(FP8X4), scales=z_scales[:, cols], in_=grouped[:])
            product(banks[c][:, :width], w3_first, z_words[:, cols], z_scales[:, cols])
            nc.scalar.activation(h_window[0][:, cols], banks[c][:, :width], ACT.Copy, scale=0.5)
            nc.scalar.activation(h_plain[0][:, cols], banks[c][:, :width], ACT.Copy, scale=0.5)
            first = first + width

        h_banks = [None, banks[3], banks[5], banks[6]]

        def project(t):
            grouped = deal(nc.vector.tensor_copy, raw3, t, "w3", staging[t])
            weights = quantise_weights(grouped, "w3_%d" % t)
            product(h_banks[t][:], weights, z_words[:], z_scales[:])

        def release(t):
            nc.scalar.activation(h_window[t][:, :S], h_banks[t][:], ACT.Copy, scale=0.5)
            nc.scalar.activation(h_plain[t], h_banks[t][:], ACT.Copy, scale=0.5)

        for t in range(1, PACK):
            project(t)

        def hinge_gather(target, t, name, cols):
            nc.vector.tensor_tensor(
                target[:, cols],
                h_window[t][:].indirect(lists[name][:, cols.start // 16 : cols.stop // 16]),
                h_plain[t][:, cols],
                ALU.subtract,
            )

        def turn(bank, terms):
            for k in range(S // P):
                block = slice(k * P, (k + 1) * P)
                for n, term in enumerate(terms):
                    nc.tensor.matmul(
                        bank[:, block], term[:, block], identity[:], is_transpose=True, start=n == 0, stop=n == len(terms) - 1
                    )

        for t in range(1, PACK):
            release(t)

        below_banks = [banks[0], banks[2]]
        above_banks = [banks[1], banks[7]]
        sum_banks = [banks[4], banks[3]]
        out_rows = out.rearrange("(b t q) c -> t b q c", t=PACK, q=RUN)
        for t in range(PACK):
            below = sb([P, S], F32, "below%d" % t)
            above = sb([P, S], F32, "above%d" % t, "above%d" % min(t, PACK - 2))
            for cols in halves if t == 0 else [slice(0, S)]:
                hinge_gather(below, t, "n3", cols)
            pieces = halves if t == PACK - 1 else [slice(0, S)]
            for cols in pieces:
                hinge_gather(above, t, "n4", cols)
            if t < TURNED:
                low = sb([P, S], F32, "low%d" % t)
                high = sb([P, S], F32, "high%d" % t)
                turn(below_banks[t], [below])
                nc.scalar.activation(low[:], below_banks[t][:], ACT.Relu, scale=-2.0)
                turn(above_banks[t], [above])
                nc.scalar.activation(high[:], above_banks[t][:], ACT.Relu)
                turn(sum_banks[t], [low, high])
            else:
                hinge = sb([P, S], F32, "hinge%d" % t)
                nc.scalar.activation(hinge[:], below[:], ACT.Relu, scale=-2.0)
                summed = sb([P, S], F32, "summed%d" % (t - TURNED))
                nc.scalar.copy(summed[:], sum_banks[t - TURNED][:])
                nc.sync.dma_start(out=out_rows[t - TURNED], in_=summed[:])
                for cols in pieces:
                    result = sb([P, cols.stop - cols.start], F32, "result%d_%d" % (t, cols.start))
                    nc.vector.scalar_tensor_tensor(result[:], above[:, cols], 0.0, hinge[:, cols], ALU.max, ALU.add)
                    nc.sync.dma_start(out=out_rows[t][:, :, cols], in_=result[:])
